import numpy as np
import ml_dtypes


def mxq(x, axis, fmt="e4m3"):
    dtype, down = {"e4m3": (ml_dtypes.float8_e4m3fn, 7), "e5m2": (ml_dtypes.float8_e5m2, 14)}[fmt]
    v = np.moveaxis(np.asarray(x, np.float32).astype(ml_dtypes.bfloat16).astype(np.float64), axis, -1)
    blocks = v.reshape(v.shape[:-1] + (-1, 32))
    amax = np.abs(blocks).max(-1, keepdims=True)
    byte = np.maximum(np.where(amax > 0, np.frexp(amax)[1] - 1 + 127, 0) - down, 1)
    scale = np.exp2(byte - 127.0)
    codes = (blocks / scale).astype(np.float32).astype(dtype).astype(np.float64)
    return np.moveaxis((codes * scale).reshape(v.shape), -1, axis)


WIDE = False


def mx_kscale(k):
    if not WIDE:
        return np.ones(k)
    levels = np.array([10, -10, 5, -5, 0])
    if k % 512:
        return np.exp2(np.random.permutation(np.resize(levels, k // 32))).repeat(32)
    a = np.empty((k // 512, 16))
    for p in range(k // 512):
        a[p, :8] = np.random.permutation(np.resize(levels, 8))
        for g in range(8):
            far = levels[np.abs(levels - a[p, g]) >= 10]
            a[p, g + 8] = far[np.random.randint(len(far))]
    return np.exp2(a.ravel()).repeat(32)


BF16 = ml_dtypes.bfloat16


def bf(x):
    return np.asarray(x, np.float32).astype(BF16)


def f64(x):
    return np.asarray(x).astype(np.float64)


E2M1 = np.array([0.0, 0.5, 1.0, 1.5, 2.0, 3.0, 4.0, 6.0, -0.0, -0.5, -1.0, -1.5, -2.0, -3.0, -4.0, -6.0])


def pack_weight(w, fmt):
    k, n = w.shape
    w = f64(bf(w)).reshape(k // 32, 32, n)
    amax = np.abs(w).max(1)
    if fmt == "e4m3":
        byte = np.frexp(amax)[1] - 1 + 127 - 7
    else:
        mant, ex = np.frexp(amax / 6.0)
        byte = np.where(mant > 0.5, ex, ex - 1) + 127
    byte = np.clip(np.where(amax > 0, byte, 1), 1, 254)
    scaled = (w * np.exp2(127.0 - byte)[:, None, :]).reshape(k, n).astype(np.float32)
    by_word = np.ascontiguousarray(scaled.reshape(k // 512, 128, 4, n).transpose(0, 1, 3, 2))
    if fmt == "e4m3":
        words = by_word.astype(ml_dtypes.float8_e4m3fn).view(np.uint8)
    else:
        c = by_word.astype(ml_dtypes.float4_e2m1fn).view(np.uint8) & 0xF
        words = c[..., 0::2] | (c[..., 1::2] << 4)
    return np.ascontiguousarray(words), np.ascontiguousarray(byte.astype(np.uint8).reshape(k // 512, 16, n))


def unpack_weight(words, scales, fmt):
    g, p, n, _ = words.shape
    if fmt == "e4m3":
        vals = np.ascontiguousarray(words).view(ml_dtypes.float8_e4m3fn).astype(np.float64)
    else:
        nib = np.empty((g, p, n, 4), np.uint8)
        nib[..., 0::2] = words & 0xF
        nib[..., 1::2] = words >> 4
        vals = E2M1[nib]
    vals = vals * np.repeat(np.exp2(scales.astype(np.float64) - 127.0), 8, axis=1)[..., None]
    return vals.transpose(0, 1, 3, 2).reshape(g * 512, n)
def pack4(w):
    words, scales = pack_weight(w, "e2m1")
    return words.reshape(words.shape[0], 128, -1), scales


def unpack4(words, scales):
    return unpack_weight(words.reshape(words.shape[0], 128, -1, 2), scales, "e2m1")


M, D = 512, 1536
HALF = 0.5


def setup_inputs():
    s, t, u = mx_kscale(D), mx_kscale(D), mx_kscale(D)
    off = (1 - np.eye(D)) / np.sqrt(2 * D)
    a1 = np.random.standard_normal((D, D))
    a2 = np.random.standard_normal((D, D))
    a3 = np.random.standard_normal((D, D))
    g1_words, g1_scales = pack4(HALF * (a1 + a1.T) * off / s[:, None] * t)
    g2_words, g2_scales = pack4(HALF * (a2 + a2.T) * off / t[:, None] * u)
    g3_words, g3_scales = pack4((a3 + a3.T) * off / u[:, None])
    return {"e0": bf(np.random.standard_normal((M, D)) * s),
            "pi1": bf((1 + 0.1 * np.random.standard_normal(D)) * t / s),
            "pi2": bf((1 + 0.1 * np.random.standard_normal(D)) * u / t),
            "g1_words": g1_words, "g1_scales": g1_scales,
            "g2_words": g2_words, "g2_scales": g2_scales,
            "g3_words": g3_words, "g3_scales": g3_scales}


def reference(e0, pi1, pi2, g1_words, g1_scales, g2_words, g2_scales, g3_words, g3_scales):
    x = f64(e0)
    c1 = mxq(x, 1, "e4m3") @ unpack4(g1_words, g1_scales)
    e1 = f64(pi1) * x - np.maximum(c1, 0)
    c2 = mxq(e1, 1, "e4m3") @ unpack4(g2_words, g2_scales)
    e2 = f64(pi2) * e1 - np.maximum(c2, 0)
    return mxq(e2, 1, "e4m3") @ unpack4(g3_words, g3_scales)

@@ -1,0 +1,271 @@
+from contextlib import ExitStack
+
+import concourse.mybir as mybir
+from concourse.masks import make_identity
+
+M, D = 512, 1536
+FLOPS = 3 * 2 * M * D * D
+
+F32 = mybir.dt.float32
+BF16 = mybir.dt.bfloat16
+I32 = mybir.dt.int32
+U32 = mybir.dt.uint32
+U8 = mybir.dt.uint8
+FP8X4 = mybir.dt.float8_e4m3fn_x4
+FP4X4 = mybir.dt.float4_e2m1fn_x4
+MAX = mybir.AluOpType.max
+MIN = mybir.AluOpType.min
+MULT = mybir.AluOpType.mult
+SUB = mybir.AluOpType.subtract
+
+P = 128
+GROUPS = D // 512
+MT = M // P
+NT = D // 512
+
+
+def tile_cortical_error_feedback_t2_kernel(
+    tc, e0, pi1, pi2, g1_words, g1_scales, g2_words, g2_scales, g3_words, g3_scales, out
+):
+    nc = tc.nc
+    with ExitStack() as ctx:
+        keep = ctx.enter_context(tc.tile_pool(name="keep", bufs=1))
+        stage = ctx.enter_context(tc.tile_pool(name="stage", bufs=3))
+        psum = ctx.enter_context(tc.psum_pool(name="psum", bufs=8))
+        ctx.enter_context(tc.manual_schedule())
+
+        words_in = (g1_words, g2_words, g3_words)
+        scales_in = (g1_scales, g2_scales, g3_scales)
+        x = [keep.tile([P, D], BF16, name=f"x{m}", align_bytes=64) for m in range(MT)]
+        words = [[keep.tile([P, 2 * D], U8, name=f"w{s}_{g}", align_bytes=64) for g in range(GROUPS)] for s in range(3)]
+        planes = [keep.tile([P, GROUPS, D], U8, name=f"plane{s}", align_bytes=64) for s in range(3)]
+        y1 = [keep.tile([P, D], F32, name=f"ya{m}") for m in range(MT)]
+        y2 = [keep.tile([P, D], F32, name=f"yb{m}") for m in range(MT)]
+        ne1 = [keep.tile([P, D], F32, name=f"ne{m}") for m in range(MT)]
+        b1 = [keep.tile([P, D], BF16, name=f"ba{m}") for m in range(MT)]
+        b2 = [keep.tile([P, D], BF16, name=f"bb{m}") for m in range(MT)]
+        pis = [keep.tile([P, GROUPS, 4], BF16, name=f"pis{i}") for i in range(2)]
+        pib = [keep.tile([P, D], BF16, name=f"pib{i}") for i in range(2)]
+        id32 = keep.tile([P, P], F32, name="id32")
+        id16 = keep.tile([P, P], BF16, name="id16")
+        warm = keep.tile([P, 2], F32, name="warm")
+
+        def bank(name):
+            return psum.tile([P, 512], F32, name=name, tag="bank")
+
+        def load_x(m):
+            nc.sync.dma_start(out=x[m][:], in_=e0[m * P : (m + 1) * P, :])
+
+        def load_words(s, g):
+            nc.sync.dma_start(out=words[s][g][:].bitcast(I32), in_=words_in[s][g].bitcast(I32))
+
+        def load_scales(s):
+            for q in range(4):
+                nc.sync.dma_start(
+                    out=planes[s][32 * q : 32 * q + 4, :, :].bitcast(I32),
+                    in_=scales_in[s][:, 4 * q : 4 * q + 4, :].rearrange("g q n -> q g n").bitcast(I32),
+                )
+
+        nc.vector.memset(warm[:], 0.0)
+        nc.vector.memset(planes[0][:].rearrange("p g n -> p (g n)").bitcast(I32), 0)
+        make_identity(nc, id32[:])
+        make_identity(nc, id16[:])
+        for i, v in enumerate((pi1, pi2)):
+            nc.scalar.dma_start(out=pis[i][:], in_=v.rearrange("(g p t) -> p g t", p=P, t=4))
+        nc.scalar.copy(out=warm[:, 1:2], in_=warm[:, 0:1])
+        for s in (1, 2):
+            nc.gpsimd.memset(planes[s][:].rearrange("p g n -> p (g n)").bitcast(I32), 0)
+        load_x(0)
+        load_scales(0)
+        load_words(0, 0)
+        load_x(1)
+        load_words(0, 1)
+        load_words(0, 2)
+        load_x(2)
+        load_x(3)
+        for s in (1, 2):
+            load_scales(s)
+            for g in range(GROUPS):
+                load_words(s, g)
+
+        operand = {}
+
+        def turn(s, ms, copiers):
+            slots = [(m, g) for m in ms for g in range(GROUPS)]
+            src = (x, b1, b2)[s]
+            grouped = stage.tile([P, len(slots) * 512], BF16, name=f"gr{s}_{ms[0]}", tag=f"gr{len(ms)}", align_bytes=64)
+            codes = keep.tile([P, len(slots) * P], U32, name=f"co{s}_{ms[0]}", align_bytes=64)
+            scales = keep.tile([P, len(slots) * P], U8, name=f"sc{s}_{ms[0]}", align_bytes=64)
+            gwords = grouped[:].bitcast(F32)
+            quants = []
+            for b in range(0, len(slots), 2):
+                part = slots[b : b + 2]
+                bk = bank(f"t{s}_{ms[0]}_{b}")
+                i = 0
+                for m, g in part:
+                    xw = src[m][:].bitcast(F32)
+                    for u in range(2):
+                        if s == 1:
+                            win = xw[:, 256 * g + 128 * u : 256 * g + 128 * (u + 1)]
+                        else:
+                            win = xw[:, 256 * g + u : 256 * (g + 1) : 2]
+                        nc.tensor.transpose(bk[:, 128 * i : 128 * (i + 1)], win, id32[:])
+                        i += 1
+                k = len(part)
+                dst = gwords[:, 256 * b : 256 * (b + k)].rearrange("p (s r u) -> p s r u", r=P, u=2)
+                frm = bk[:, : 256 * k].rearrange("p (s u r) -> p s r u", u=2, r=P)
+                if copiers[b // 2] == "S":
+                    nc.scalar.copy(out=dst, in_=frm)
+                else:
+                    nc.vector.tensor_copy(out=dst, in_=frm)
+                quants.append((b, k))
+                for j, key in enumerate(part):
+                    c = slice((b + j) * P, (b + j + 1) * P)
+                    operand[(s,) + key] = (codes[:, c], scales[:, c])
+
+            def quantise(q):
+                b, k = quants[q]
+                nc.vector.quantize_mx(
+                    out=codes[:, b * P : (b + k) * P].bitcast(FP8X4),
+                    scales=scales[:, b * P : (b + k) * P],
+                    in_=grouped[:, 512 * b : 512 * (b + k)],
+                )
+
+            return [lambda q=q: quantise(q) for q in range(len(quants))]
+
+        def spread_pi(i):
+            for g0, gn in ((0, 2), (2, 1)):
+                bk = psum.tile([P, 1024], BF16, name=f"pi{i}_{g0}", tag="bank")
+                for j in range(gn):
+                    for t in range(4):
+                        o = 512 * j + 128 * t
+                        nc.tensor.transpose(
+                            bk[:, o : o + 128], pis[i][:, g0 + j, t : t + 1].to_broadcast([P, P]), id16[:]
+                        )
+                nc.scalar.copy(
+                    out=pib[i][:, 512 * g0 : 512 * (g0 + gn)].rearrange("q (j p t) -> q j p t", p=P, t=4),
+                    in_=bk[:, : 512 * gn].rearrange("q (j t p) -> q j p t", t=4, p=P),
+                )
+
+        def one_pass(acc, s, m, n, g):
+            lhs, lhs_s = operand[(s, m, g)]
+            nc.tensor.matmul_mx(
+                out=acc[:],
+                lhsT=lhs.bitcast(FP8X4),
+                lhsT_scale=lhs_s,
+                rhs=words[s][g][:, 1024 * n : 1024 * (n + 1)].bitcast(FP4X4),
+                rhs_scale=planes[s][:, g, 512 * n : 512 * (n + 1)],
+                start=(g == 0),
+                stop=(g == GROUPS - 1),
+            )
+
+        def product(s, m, by_group=False):
+            accs = [bank(f"acc{s}_{m}_{n}") for n in range(NT)]
+            if by_group:
+                order = [(g, n) for g in range(GROUPS) for n in range(NT)]
+            else:
+                order = [(g, n) for n in range(NT) for g in range(GROUPS)]
+            for g, n in order:
+                one_pass(accs[n], s, m, n, g)
+            return accs
+
+        def cols(n):
+            return slice(512 * n, 512 * (n + 1))
+
+        def mul1(eng, m, n):
+            eng.tensor_tensor(out=y1[m][:, cols(n)], in0=x[m][:, cols(n)], in1=pib[0][:, cols(n)], op=MULT)
+
+        def mul2(eng, m, n):
+            eng.tensor_tensor(out=y2[m][:, cols(n)], in0=ne1[m][:, cols(n)], in1=pib[1][:, cols(n)], op=MULT)
+
+        def epi1(accs, m):
+            for n in range(NT):
+                nc.vector.scalar_tensor_tensor(
+                    out=ne1[m][:, cols(n)], in0=accs[n][:], scalar=0.0, in1=y1[m][:, cols(n)], op0=MAX, op1=SUB
+                )
+                nc.scalar.copy(
+                    out=b1[m][:, cols(n)].rearrange("q (u p e) -> q u p e", u=2, e=2),
+                    in_=ne1[m][:, cols(n)].rearrange("q (p u e) -> q u p e", u=2, e=2),
+                )
+
+        def epi2(accs, m):
+            for n in range(NT):
+                nc.vector.scalar_tensor_tensor(
+                    out=b2[m][:, cols(n)], in0=accs[n][:], scalar=0.0, in1=y2[m][:, cols(n)], op0=MIN, op1=SUB
+                )
+
+        def epi3(accs, m, engines):
+            for n in range(NT):
+                res = stage.tile([P, 512], F32, name=f"res{m}_{n}", tag="res", bufs=6)
+                if engines[n] == "S":
+                    nc.scalar.copy(out=res[:], in_=accs[n][:])
+                    nc.sync.dma_start(out=out[m * P : (m + 1) * P, cols(n)], in_=res[:])
+                elif engines[n] == "V":
+                    nc.vector.tensor_copy(out=res[:], in_=accs[n][:])
+                    nc.sync.dma_start(out=out[m * P : (m + 1) * P, cols(n)], in_=res[:])
+                else:
+                    nc.vector.tensor_copy(out=res[:, :256], in_=accs[n][:, :256])
+                    nc.scalar.copy(out=res[:, 256:], in_=accs[n][:, 256:])
+                    nc.sync.dma_start(out=out[m * P : (m + 1) * P, cols(n)], in_=res[:])
+
+        def run(steps):
+            for step in steps:
+                step()
+
+        G, V = nc.gpsimd, nc.vector
+        q0 = turn(0, [0], "SV")
+        run(q0)
+        spread_pi(0)
+        q1 = turn(0, [1], "SV")
+        for n in range(NT):
+            mul1(V, 0, n)
+        run(q1)
+        for m in (1, 2, 3):
+            for n in range(NT):
+                mul1(G, m, n)
+        acc = product(0, 0, by_group=True)
+        epi1(acc, 0)
+        spread_pi(1)
+        q2 = turn(0, [2], "SS")
+        run(q2)
+        acc = product(0, 1)
+        epi1(acc, 1)
+        q3 = turn(0, [3], "SS")
+        run(q3)
+        acc = product(0, 2)
+        epi1(acc, 2)
+        q = turn(1, [0, 1], "SSS")
+        mul2(V, 0, 0)
+        mul2(V, 0, 1)
+        run(q)
+        mul2(V, 0, 2)
+        acc = product(0, 3)
+        epi1(acc, 3)
+        for m in (2, 3):
+            for n in range(NT):
+                mul2(G, m, n)
+        acc = product(1, 0)
+        epi2(acc, 0)
+        q = turn(1, [2, 3], "SSS")
+        mul2(V, 1, 0)
+        mul2(V, 1, 1)
+        run(q)
+        mul2(V, 1, 2)
+        acc = product(1, 1)
+        epi2(acc, 1)
+        acc = product(1, 2)
+        epi2(acc, 2)
+        q = turn(2, [0, 1], "SSS")
+        run(q)
+        acc = product(1, 3)
+        epi2(acc, 3)
+        acc = product(2, 0)
+        epi3(acc, 0, "SVS")
+        q = turn(2, [2, 3], "SSS")
+        run(q)
+        acc = product(2, 1)
+        epi3(acc, 1, "VSV")
+        acc = product(2, 2)
+        epi3(acc, 2, "SVS")
+        acc = product(2, 3)
+        epi3(acc, 3, "VSB")

@@ -23,6 +23,23 @@ GROUPS = D // 512
 MT = M // P
 NT = D // 512
 
+PI_ROWS = D // (2 * P)
+
+ORDER = """
+picol Ta cpc pi0a cTa pi0b qTa cpia Tb cpib ya00 H0_0 ya01 cTb ya02 qTb H0_1 ya10 re1 ya11 H0_2 ya12 re2 T0_1
+s1_00 s1_01 c0_1a T0_2 ya20 c0_1b c0_2a q0_1a q0_1b s1_02 c0_2b M0_1_0 ca00 ya21 ca01 q0_2a M0_1_1 q0_2b ca02
+ya22 M0_1_2 s1_10 re3 ya30 T1_0 s1_11 T0_3 c1_0a ya31 M0_2_0 c1_0b s1_12 ca10 M0_2_1 ya32 c0_3a q1_0a c0_3b
+M0_2_2 q1_0b q0_3a ca11 q0_3b s1_20 ca12 M0_3_0 s1_21 ca20 M0_3_1 s1_22 ca21 yb00 ca22 M0_3_2 s1_30 M1_0_0
+yb01 ca30 s1_31 M1_0_1 yb02 ca31 M1_0_2 s1_32 s2_00 ca32 T1_2 s2_01 T1_1 c1_2a s2_02 T1_3 c1_2b q1_2a T2_0
+c1_1a q1_2b yb20 c1_1b M1_2_0 c1_3a q1_1a q1_1b yb21 c1_3b M1_2_1 c2_0a q1_3a c2_0b q1_3b M1_2_2 yb22 q2_0a
+M1_3_0 q2_0b yb30 s2_20 M1_3_1 yb31 M1_3_2 s2_21 M2_0_0 yb32 s2_22 M2_0_1 o00 s2_30 M2_0_2 s2_31 o01 s2_32
+T2_2 o02 yb10 T2_3 c2_2a yb11 M1_1_0 c2_2b q2_2a c2_3a q2_2b M1_1_1 yb12 c2_3b q2_3a M1_1_2 q2_3b s2_10
+M2_3_0 s2_11 s2_12 M2_3_1 o30 M2_3_2 o31 T2_1 o32 M2_2_0 c2_1a c2_1b q2_1a M2_2_1 o20 q2_1b M2_2_2 o21 M2_1_0
+o22 M2_1_1 o10 M2_1_2 o11 oV oS
+"""
+ENGINE = {"o00": "S", "o01": "S", "o02": "S", "o10": "S", "o11": "S", "o20": "S", "o22": "S", "o31": "S", "o32": "S"}
+LAST = (2, 1, 2)
+
 
 def tile_cortical_error_feedback_t2_kernel(
     tc, e0, pi1, pi2, g1_words, g1_scales, g2_words, g2_scales, g3_words, g3_scales, out
@@ -30,242 +47,271 @@ def tile_cortical_error_feedback_t2_kernel(
     nc = tc.nc
     with ExitStack() as ctx:
         keep = ctx.enter_context(tc.tile_pool(name="keep", bufs=1))
-        stage = ctx.enter_context(tc.tile_pool(name="stage", bufs=3))
+        stage = ctx.enter_context(tc.tile_pool(name="stage", bufs=6))
         psum = ctx.enter_context(tc.psum_pool(name="psum", bufs=8))
         ctx.enter_context(tc.manual_schedule())
 
         words_in = (g1_words, g2_words, g3_words)
         scales_in = (g1_scales, g2_scales, g3_scales)
-        x = [keep.tile([P, D], BF16, name=f"x{m}", align_bytes=64) for m in range(MT)]
+
+        def rows(name, dtype, width=D):
+            return [keep.tile([P, width], dtype, name=f"{name}{m}", align_bytes=64) for m in range(MT)]
+
+        x = rows("x", BF16)
+        xr = rows("xr", BF16)
+        y1 = rows("ya", F32)
+        y2 = rows("yb", F32)
+        ne1 = rows("ne", F32)
+        b1 = rows("ba", BF16)
+        b2 = rows("bb", BF16)
+        grouped = [[None] * MT for s in range(3)]
+        codes = [rows(f"co{s}_", U32, 3 * P) for s in range(3)]
+        cscales = [rows(f"sc{s}_", U8, 3 * P) for s in range(3)]
         words = [[keep.tile([P, 2 * D], U8, name=f"w{s}_{g}", align_bytes=64) for g in range(GROUPS)] for s in range(3)]
         planes = [keep.tile([P, GROUPS, D], U8, name=f"plane{s}", align_bytes=64) for s in range(3)]
-        y1 = [keep.tile([P, D], F32, name=f"ya{m}") for m in range(MT)]
-        y2 = [keep.tile([P, D], F32, name=f"yb{m}") for m in range(MT)]
-        ne1 = [keep.tile([P, D], F32, name=f"ne{m}") for m in range(MT)]
-        b1 = [keep.tile([P, D], BF16, name=f"ba{m}") for m in range(MT)]
-        b2 = [keep.tile([P, D], BF16, name=f"bb{m}") for m in range(MT)]
-        pis = [keep.tile([P, GROUPS, 4], BF16, name=f"pis{i}") for i in range(2)]
+        pirow = keep.tile([P, 2 * P], BF16, name="pirow")
+        picol = keep.tile([P, PI_ROWS], F32, name="picol")
         pib = [keep.tile([P, D], BF16, name=f"pib{i}") for i in range(2)]
         id32 = keep.tile([P, P], F32, name="id32")
-        id16 = keep.tile([P, P], BF16, name="id16")
         warm = keep.tile([P, 2], F32, name="warm")
 
-        def bank(name):
-            return psum.tile([P, 512], F32, name=name, tag="bank")
-
-        def load_x(m):
-            nc.sync.dma_start(out=x[m][:], in_=e0[m * P : (m + 1) * P, :])
+        def load_x(m, c0=0, c1=D):
+            nc.sync.dma_start(out=x[m][:, c0:c1], in_=e0[m * P : (m + 1) * P, c0:c1])
 
         def load_words(s, g):
             nc.sync.dma_start(out=words[s][g][:].bitcast(I32), in_=words_in[s][g].bitcast(I32))
 
-        def load_scales(s):
+        def load_scales(s, g0=0, g1=GROUPS):
             for q in range(4):
                 nc.sync.dma_start(
-                    out=planes[s][32 * q : 32 * q + 4, :, :].bitcast(I32),
-                    in_=scales_in[s][:, 4 * q : 4 * q + 4, :].rearrange("g q n -> q g n").bitcast(I32),
+                    out=planes[s][32 * q : 32 * q + 4, g0:g1, :].bitcast(I32),
+                    in_=scales_in[s][g0:g1, 4 * q : 4 * q + 4, :].rearrange("g q n -> q g n").bitcast(I32),
                 )
 
+        nc.vector.memset(pirow[:], 0.0)
         nc.vector.memset(warm[:], 0.0)
         nc.vector.memset(planes[0][:].rearrange("p g n -> p (g n)").bitcast(I32), 0)
         make_identity(nc, id32[:])
-        make_identity(nc, id16[:])
-        for i, v in enumerate((pi1, pi2)):
-            nc.scalar.dma_start(out=pis[i][:], in_=v.rearrange("(g p t) -> p g t", p=P, t=4))
+        nc.scalar.dma_start(out=pirow[0:PI_ROWS, :], in_=pi1.rearrange("(r c) -> r c", c=2 * P))
         nc.scalar.copy(out=warm[:, 1:2], in_=warm[:, 0:1])
         for s in (1, 2):
             nc.gpsimd.memset(planes[s][:].rearrange("p g n -> p (g n)").bitcast(I32), 0)
-        load_x(0)
-        load_scales(0)
+        load_x(0, 0, 512)
+        load_x(0, 512, D)
+        load_scales(0, 0, 1)
         load_words(0, 0)
-        load_x(1)
+        load_scales(0, 1, 3)
         load_words(0, 1)
+        load_x(1)
         load_words(0, 2)
         load_x(2)
+        load_scales(1)
+        for g in range(GROUPS):
+            load_words(1, g)
         load_x(3)
-        for s in (1, 2):
-            load_scales(s)
-            for g in range(GROUPS):
-                load_words(s, g)
+        nc.sync.dma_start(out=pib[1][:], in_=pi2.partition_broadcast(P))
+        load_scales(2)
+        for g in range(GROUPS):
+            load_words(2, g)
 
-        operand = {}
+        banks = {}
 
-        def turn(s, ms, copiers):
-            slots = [(m, g) for m in ms for g in range(GROUPS)]
-            src = (x, b1, b2)[s]
-            grouped = stage.tile([P, len(slots) * 512], BF16, name=f"gr{s}_{ms[0]}", tag=f"gr{len(ms)}", align_bytes=64)
-            codes = keep.tile([P, len(slots) * P], U32, name=f"co{s}_{ms[0]}", align_bytes=64)
-            scales = keep.tile([P, len(slots) * P], U8, name=f"sc{s}_{ms[0]}", align_bytes=64)
-            gwords = grouped[:].bitcast(F32)
-            quants = []
-            for b in range(0, len(slots), 2):
-                part = slots[b : b + 2]
-                bk = bank(f"t{s}_{ms[0]}_{b}")
-                i = 0
-                for m, g in part:
-                    xw = src[m][:].bitcast(F32)
-                    for u in range(2):
-                        if s == 1:
-                            win = xw[:, 256 * g + 128 * u : 256 * g + 128 * (u + 1)]
-                        else:
-                            win = xw[:, 256 * g + u : 256 * (g + 1) : 2]
-                        nc.tensor.transpose(bk[:, 128 * i : 128 * (i + 1)], win, id32[:])
-                        i += 1
-                k = len(part)
-                dst = gwords[:, 256 * b : 256 * (b + k)].rearrange("p (s r u) -> p s r u", r=P, u=2)
-                frm = bk[:, : 256 * k].rearrange("p (s u r) -> p s r u", u=2, r=P)
-                if copiers[b // 2] == "S":
-                    nc.scalar.copy(out=dst, in_=frm)
-                else:
-                    nc.vector.tensor_copy(out=dst, in_=frm)
-                quants.append((b, k))
-                for j, key in enumerate(part):
-                    c = slice((b + j) * P, (b + j + 1) * P)
-                    operand[(s,) + key] = (codes[:, c], scales[:, c])
-
-            def quantise(q):
-                b, k = quants[q]
-                nc.vector.quantize_mx(
-                    out=codes[:, b * P : (b + k) * P].bitcast(FP8X4),
-                    scales=scales[:, b * P : (b + k) * P],
-                    in_=grouped[:, 512 * b : 512 * (b + k)],
-                )
-
-            return [lambda q=q: quantise(q) for q in range(len(quants))]
-
-        def spread_pi(i):
-            for g0, gn in ((0, 2), (2, 1)):
-                bk = psum.tile([P, 1024], BF16, name=f"pi{i}_{g0}", tag="bank")
-                for j in range(gn):
-                    for t in range(4):
-                        o = 512 * j + 128 * t
-                        nc.tensor.transpose(
-                            bk[:, o : o + 128], pis[i][:, g0 + j, t : t + 1].to_broadcast([P, P]), id16[:]
-                        )
-                nc.scalar.copy(
-                    out=pib[i][:, 512 * g0 : 512 * (g0 + gn)].rearrange("q (j p t) -> q j p t", p=P, t=4),
-                    in_=bk[:, : 512 * gn].rearrange("q (j t p) -> q j p t", t=4, p=P),
-                )
-
-        def one_pass(acc, s, m, n, g):
-            lhs, lhs_s = operand[(s, m, g)]
-            nc.tensor.matmul_mx(
-                out=acc[:],
-                lhsT=lhs.bitcast(FP8X4),
-                lhsT_scale=lhs_s,
-                rhs=words[s][g][:, 1024 * n : 1024 * (n + 1)].bitcast(FP4X4),
-                rhs_scale=planes[s][:, g, 512 * n : 512 * (n + 1)],
-                start=(g == 0),
-                stop=(g == GROUPS - 1),
-            )
-
-        def product(s, m, by_group=False):
-            accs = [bank(f"acc{s}_{m}_{n}") for n in range(NT)]
-            if by_group:
-                order = [(g, n) for g in range(GROUPS) for n in range(NT)]
-            else:
-                order = [(g, n) for n in range(NT) for g in range(GROUPS)]
-            for g, n in order:
-                one_pass(accs[n], s, m, n, g)
-            return accs
+        def bank(key, dtype=F32):
+            banks[key] = psum.tile([P, 512 if dtype == F32 else 1024], dtype, name=f"b_{key}", tag="bank")
+            return banks[key]
 
         def cols(n):
             return slice(512 * n, 512 * (n + 1))
 
-        def mul1(eng, m, n):
-            eng.tensor_tensor(out=y1[m][:, cols(n)], in0=x[m][:, cols(n)], in1=pib[0][:, cols(n)], op=MULT)
+        def words_up(s, m, g, u):
+            if s == 0 and m == 0:
+                return x[m][:].bitcast(F32)[:, 256 * g + u : 256 * (g + 1) : 2]
+            src = (xr, b1, b2)[s][m]
+            return src[:].bitcast(F32)[:, 256 * g + 128 * u : 256 * g + 128 * (u + 1)]
 
-        def mul2(eng, m, n):
-            eng.tensor_tensor(out=y2[m][:, cols(n)], in0=ne1[m][:, cols(n)], in1=pib[1][:, cols(n)], op=MULT)
+        def turn(s, m, groups, key):
+            if groups[0] == 0:
+                grouped[s][m] = stage.tile([P, 12 * P], BF16, name=f"gr{s}_{m}", tag="gr", align_bytes=64)
+            bk = bank(key)
+            for i, (g, u) in enumerate([(g, u) for g in groups for u in range(2)]):
+                nc.tensor.transpose(bk[:, P * i : P * (i + 1)], words_up(s, m, g, u), id32[:])
 
-        def epi1(accs, m):
-            for n in range(NT):
+        def turn_out(s, m, groups, key, copy_on):
+            k = len(groups)
+            dst = grouped[s][m][:].bitcast(F32)[:, 256 * groups[0] : 256 * (groups[0] + k)]
+            dst = dst.rearrange("p (s r u) -> p s r u", r=P, u=2)
+            src = banks[key][:, : 256 * k].rearrange("p (s u r) -> p s r u", u=2, r=P)
+            if copy_on == "S":
+                nc.scalar.copy(out=dst, in_=src)
+            else:
+                nc.vector.tensor_copy(out=dst, in_=src)
+
+        def quantise(s, m, groups):
+            g, k = groups[0], len(groups)
+            nc.vector.quantize_mx(
+                out=codes[s][m][:, g * P : (g + k) * P].bitcast(FP8X4),
+                scales=cscales[s][m][:, g * P : (g + k) * P],
+                in_=grouped[s][m][:, 512 * g : 512 * (g + k)],
+            )
+
+        def one_pass(acc, s, m, n, g):
+            nc.tensor.matmul_mx(
+                out=acc[:],
+                lhsT=codes[s][m][:, g * P : (g + 1) * P].bitcast(FP8X4),
+                lhsT_scale=cscales[s][m][:, g * P : (g + 1) * P],
+                rhs=words[s][g][:, 1024 * n : 1024 * (n + 1)].bitcast(FP4X4),
+                rhs_scale=planes[s][:, g, cols(n)],
+                start=(g == 0),
+                stop=(g == GROUPS - 1),
+            )
+
+        def reorder(m):
+            nc.scalar.copy(
+                out=xr[m][:].bitcast(F32).rearrange("q (g u p) -> q g u p", g=GROUPS, u=2),
+                in_=x[m][:].bitcast(F32).rearrange("q (g p u) -> q g u p", g=GROUPS, u=2),
+            )
+
+        def pi_columns():
+            nc.tensor.transpose(bank("picol")[:, :P], pirow[:].bitcast(F32), id32[:])
+
+        def pi_spread(key, r0, rn):
+            bk = bank(key)
+            for j in range(rn):
+                c = r0 + j
+                nc.tensor.transpose(bk[:, P * j : P * (j + 1)], picol[:, c : c + 1].to_broadcast([P, P]), id32[:])
+
+        def pi_out(key, r0, rn):
+            nc.scalar.copy(out=pib[0][:].bitcast(F32)[:, P * r0 : P * (r0 + rn)], in_=banks[key][:, : P * rn])
+
+        def mul(eng, y, a, b, n):
+            eng.tensor_tensor(out=y[:, cols(n)], in0=a[:, cols(n)], in1=b[:, cols(n)], op=MULT)
+
+        def epi1(m, n):
+            nc.vector.scalar_tensor_tensor(
+                out=ne1[m][:, cols(n)], in0=banks[(1, m, n)][:], scalar=0.0, in1=y1[m][:, cols(n)], op0=MAX, op1=SUB
+            )
+
+        def cast1(m, n):
+            nc.scalar.copy(
+                out=b1[m][:, cols(n)].rearrange("q (u p e) -> q u p e", u=2, e=2),
+                in_=ne1[m][:, cols(n)].rearrange("q (p u e) -> q u p e", u=2, e=2),
+            )
+
+        def epi2(m, n):
+            acc = banks[(2, m, n)][:].rearrange("q (p u e) -> q u p e", u=2, e=2)
+            y = y2[m][:, cols(n)].rearrange("q (p u e) -> q u p e", u=2, e=2)
+            for u in range(2):
+                c = 512 * n + 256 * u
                 nc.vector.scalar_tensor_tensor(
-                    out=ne1[m][:, cols(n)], in0=accs[n][:], scalar=0.0, in1=y1[m][:, cols(n)], op0=MAX, op1=SUB
-                )
-                nc.scalar.copy(
-                    out=b1[m][:, cols(n)].rearrange("q (u p e) -> q u p e", u=2, e=2),
-                    in_=ne1[m][:, cols(n)].rearrange("q (p u e) -> q u p e", u=2, e=2),
-                )
-
-        def epi2(accs, m):
-            for n in range(NT):
-                nc.vector.scalar_tensor_tensor(
-                    out=b2[m][:, cols(n)], in0=accs[n][:], scalar=0.0, in1=y2[m][:, cols(n)], op0=MIN, op1=SUB
+                    out=b2[m][:, c : c + 256].rearrange("q (p e) -> q p e", e=2),
+                    in0=acc[:, u],
+                    scalar=0.0,
+                    in1=y[:, u],
+                    op0=MIN,
+                    op1=SUB,
                 )
 
-        def epi3(accs, m, engines):
-            for n in range(NT):
-                res = stage.tile([P, 512], F32, name=f"res{m}_{n}", tag="res", bufs=6)
-                if engines[n] == "S":
-                    nc.scalar.copy(out=res[:], in_=accs[n][:])
-                    nc.sync.dma_start(out=out[m * P : (m + 1) * P, cols(n)], in_=res[:])
-                elif engines[n] == "V":
-                    nc.vector.tensor_copy(out=res[:], in_=accs[n][:])
-                    nc.sync.dma_start(out=out[m * P : (m + 1) * P, cols(n)], in_=res[:])
-                else:
-                    nc.vector.tensor_copy(out=res[:, :256], in_=accs[n][:, :256])
-                    nc.scalar.copy(out=res[:, 256:], in_=accs[n][:, 256:])
-                    nc.sync.dma_start(out=out[m * P : (m + 1) * P, cols(n)], in_=res[:])
+        res = {}
 
-        def run(steps):
-            for step in steps:
-                step()
+        def epi3(m, n, c0, c1, eng, last):
+            if (m, n) not in res:
+                res[(m, n)] = stage.tile([P, 512], F32, name=f"res{m}_{n}", tag="res")
+            r = res[(m, n)]
+            if eng == "S":
+                nc.scalar.copy(out=r[:, c0:c1], in_=banks[(3, m, n)][:, c0:c1])
+            else:
+                nc.vector.tensor_copy(out=r[:, c0:c1], in_=banks[(3, m, n)][:, c0:c1])
+            if last:
+                nc.sync.dma_start(out=out[m * P : (m + 1) * P, cols(n)], in_=r[:])
 
-        G, V = nc.gpsimd, nc.vector
-        q0 = turn(0, [0], "SV")
-        run(q0)
-        spread_pi(0)
-        q1 = turn(0, [1], "SV")
-        for n in range(NT):
-            mul1(V, 0, n)
-        run(q1)
-        for m in (1, 2, 3):
+        def last_product(m, n):
+            for h in range(2):
+                acc = bank((3, m, n, h))
+                for q in range(2):
+                    c = 512 * n + 256 * h + P * q
+                    for g in range(GROUPS):
+                        nc.tensor.matmul_mx(
+                            out=acc[:, P * q : P * (q + 1)],
+                            lhsT=codes[2][m][:, g * P : (g + 1) * P].bitcast(FP8X4),
+                            lhsT_scale=cscales[2][m][:, g * P : (g + 1) * P],
+                            rhs=words[2][g][:, 2 * c : 2 * (c + P)].bitcast(FP4X4),
+                            rhs_scale=planes[2][:, g, c : c + P],
+                            start=(g == 0),
+                            stop=(g == GROUPS - 1),
+                        )
+
+        def last_out(m, n, step):
+            if step == 0:
+                r = stage.tile([P, 256], F32, name="last0", tag="last")
+                nc.vector.tensor_copy(out=r[:], in_=banks[(3, m, n, 0)][:, :256])
+                nc.sync.dma_start(out=out[m * P : (m + 1) * P, 512 * n : 512 * n + 256], in_=r[:])
+                res["last"] = stage.tile([P, 256], F32, name="last1", tag="last")
+                nc.vector.tensor_copy(out=res["last"][:, :P], in_=banks[(3, m, n, 1)][:, :P])
+            else:
+                nc.scalar.copy(out=res["last"][:, P:], in_=banks[(3, m, n, 1)][:, P:256])
+                nc.sync.dma_start(out=out[m * P : (m + 1) * P, 512 * n + 256 : 512 * n + 512], in_=res["last"][:])
+
+        def product(s, m, n):
+            if (s, m, n) == LAST:
+                last_product(m, n)
+                return
+            acc = bank((s + 1, m, n))
+            for g in range(GROUPS):
+                one_pass(acc, s, m, n, g)
+
+        def head(g):
             for n in range(NT):
-                mul1(G, m, n)
-        acc = product(0, 0, by_group=True)
-        epi1(acc, 0)
-        spread_pi(1)
-        q2 = turn(0, [2], "SS")
-        run(q2)
-        acc = product(0, 1)
-        epi1(acc, 1)
-        q3 = turn(0, [3], "SS")
-        run(q3)
-        acc = product(0, 2)
-        epi1(acc, 2)
-        q = turn(1, [0, 1], "SSS")
-        mul2(V, 0, 0)
-        mul2(V, 0, 1)
-        run(q)
-        mul2(V, 0, 2)
-        acc = product(0, 3)
-        epi1(acc, 3)
-        for m in (2, 3):
-            for n in range(NT):
-                mul2(G, m, n)
-        acc = product(1, 0)
-        epi2(acc, 0)
-        q = turn(1, [2, 3], "SSS")
-        mul2(V, 1, 0)
-        mul2(V, 1, 1)
-        run(q)
-        mul2(V, 1, 2)
-        acc = product(1, 1)
-        epi2(acc, 1)
-        acc = product(1, 2)
-        epi2(acc, 2)
-        q = turn(2, [0, 1], "SSS")
-        run(q)
-        acc = product(1, 3)
-        epi2(acc, 3)
-        acc = product(2, 0)
-        epi3(acc, 0, "SVS")
-        q = turn(2, [2, 3], "SSS")
-        run(q)
-        acc = product(2, 1)
-        epi3(acc, 1, "VSV")
-        acc = product(2, 2)
-        epi3(acc, 2, "SVS")
-        acc = product(2, 3)
-        epi3(acc, 3, "VSB")
+                if g == 0:
+                    bank((1, 0, n))
+                one_pass(banks[(1, 0, n)], 0, 0, n, g)
+
+        def do(name):
+            if name == "picol":
+                pi_columns()
+            elif name == "cpc":
+                nc.scalar.copy(out=picol[:], in_=banks["picol"][:, :PI_ROWS])
+            elif name in ("pi0a", "pi0b"):
+                pi_spread(name, *((0, 4) if name == "pi0a" else (4, 2)))
+            elif name in ("cpia", "cpib"):
+                pi_out("pi0" + name[3], *((0, 4) if name == "cpia" else (4, 2)))
+            elif name in ("Ta", "Tb"):
+                turn(0, 0, [0] if name == "Ta" else [1, 2], name)
+            elif name in ("cTa", "cTb"):
+                turn_out(0, 0, [0] if name == "cTa" else [1, 2], name[1:], ENGINE.get(name, "S"))
+            elif name in ("qTa", "qTb"):
+                quantise(0, 0, [0] if name == "qTa" else [1, 2])
+            elif name.startswith("re"):
+                reorder(int(name[2]))
+            elif name.startswith("H"):
+                head(int(name[3]))
+            elif name.startswith("M"):
+                product(*[int(v) for v in name[1:].split("_")])
+            elif name.startswith("T"):
+                s, m = int(name[1]), int(name[3])
+                turn(s, m, [0, 1], name + "a")
+                turn(s, m, [2], name + "b")
+            elif name.startswith("ca"):
+                cast1(int(name[2]), int(name[3]))
+            elif name.startswith("c"):
+                turn_out(int(name[1]), int(name[3]), [0, 1] if name[4] == "a" else [2], "T" + name[1:], ENGINE.get(name, "S"))
+            elif name.startswith("q"):
+                quantise(int(name[1]), int(name[3]), [0, 1] if name[4] == "a" else [2])
+            elif name.startswith("ya"):
+                m, n = int(name[2]), int(name[3])
+                mul(nc.gpsimd if name in ENGINE else nc.vector, y1[m], x[m], pib[0], n)
+            elif name.startswith("yb"):
+                m, n = int(name[2]), int(name[3])
+                mul(nc.gpsimd if name in ENGINE else nc.vector, y2[m], ne1[m], pib[1], n)
+            elif name.startswith("s1"):
+                epi1(int(name[3]), int(name[4]))
+            elif name.startswith("s2"):
+                epi2(int(name[3]), int(name[4]))
+            elif name == "oS":
+                last_out(LAST[1], LAST[2], 1)
+            elif name == "oV":
+                last_out(LAST[1], LAST[2], 0)
+            else:
+                epi3(int(name[1]), int(name[2]), 0, 512, ENGINE.get(name, "V"), True)
+
+        for name in ORDER.split():
+            do(name)

from contextlib import ExitStack

import concourse.mybir as mybir
from concourse.masks import make_identity

M, D = 512, 1536
FLOPS = 3 * 2 * M * D * D

F32 = mybir.dt.float32
BF16 = mybir.dt.bfloat16
I32 = mybir.dt.int32
U32 = mybir.dt.uint32
U8 = mybir.dt.uint8
FP8X4 = mybir.dt.float8_e4m3fn_x4
FP4X4 = mybir.dt.float4_e2m1fn_x4
MAX = mybir.AluOpType.max
MIN = mybir.AluOpType.min
MULT = mybir.AluOpType.mult
SUB = mybir.AluOpType.subtract

P = 128
GROUPS = D // 512
MT = M // P
NT = D // 512

PI_ROWS = D // (2 * P)

ORDER = """
picol Ta cpc pi0a cTa pi0b qTa cpia Tb cpib ya00 H0_0 ya01 cTb ya02 qTb H0_1 ya10 re1 ya11 H0_2 ya12 re2 T0_1
s1_00 s1_01 c0_1a T0_2 ya20 c0_1b c0_2a q0_1a q0_1b s1_02 c0_2b M0_1_0 ca00 ya21 ca01 q0_2a M0_1_1 q0_2b ca02
ya22 M0_1_2 s1_10 re3 ya30 T1_0 s1_11 T0_3 c1_0a ya31 M0_2_0 c1_0b s1_12 ca10 M0_2_1 ya32 c0_3a q1_0a c0_3b
M0_2_2 q1_0b q0_3a ca11 q0_3b s1_20 ca12 M0_3_0 s1_21 ca20 M0_3_1 s1_22 ca21 yb00 ca22 M0_3_2 s1_30 M1_0_0
yb01 ca30 s1_31 M1_0_1 yb02 ca31 M1_0_2 s1_32 s2_00 ca32 T1_2 s2_01 T1_1 c1_2a s2_02 T1_3 c1_2b q1_2a T2_0
c1_1a q1_2b yb20 c1_1b M1_2_0 c1_3a q1_1a q1_1b yb21 c1_3b M1_2_1 c2_0a q1_3a c2_0b q1_3b M1_2_2 yb22 q2_0a
M1_3_0 q2_0b yb30 s2_20 M1_3_1 yb31 M1_3_2 s2_21 M2_0_0 yb32 s2_22 M2_0_1 o00 s2_30 M2_0_2 s2_31 o01 s2_32
T2_2 o02 yb10 T2_3 c2_2a yb11 M1_1_0 c2_2b q2_2a c2_3a q2_2b M1_1_1 yb12 c2_3b q2_3a M1_1_2 q2_3b s2_10
M2_3_0 s2_11 s2_12 M2_3_1 o30 M2_3_2 o31 T2_1 o32 M2_2_0 c2_1a c2_1b q2_1a M2_2_1 o20 q2_1b M2_2_2 o21 M2_1_0
o22 M2_1_1 o10 M2_1_2 o11 oV oS
"""
ENGINE = {"o00": "S", "o01": "S", "o02": "S", "o10": "S", "o11": "S", "o20": "S", "o22": "S", "o31": "S", "o32": "S"}
LAST = (2, 1, 2)


def tile_cortical_error_feedback_t2_kernel(
    tc, e0, pi1, pi2, g1_words, g1_scales, g2_words, g2_scales, g3_words, g3_scales, out
):
    nc = tc.nc
    with ExitStack() as ctx:
        keep = ctx.enter_context(tc.tile_pool(name="keep", bufs=1))
        stage = ctx.enter_context(tc.tile_pool(name="stage", bufs=6))
        psum = ctx.enter_context(tc.psum_pool(name="psum", bufs=8))
        ctx.enter_context(tc.manual_schedule())

        words_in = (g1_words, g2_words, g3_words)
        scales_in = (g1_scales, g2_scales, g3_scales)

        def rows(name, dtype, width=D):
            return [keep.tile([P, width], dtype, name=f"{name}{m}", align_bytes=64) for m in range(MT)]

        x = rows("x", BF16)
        xr = rows("xr", BF16)
        y1 = rows("ya", F32)
        y2 = rows("yb", F32)
        ne1 = rows("ne", F32)
        b1 = rows("ba", BF16)
        b2 = rows("bb", BF16)
        grouped = [[None] * MT for s in range(3)]
        codes = [rows(f"co{s}_", U32, 3 * P) for s in range(3)]
        cscales = [rows(f"sc{s}_", U8, 3 * P) for s in range(3)]
        words = [[keep.tile([P, 2 * D], U8, name=f"w{s}_{g}", align_bytes=64) for g in range(GROUPS)] for s in range(3)]
        planes = [keep.tile([P, GROUPS, D], U8, name=f"plane{s}", align_bytes=64) for s in range(3)]
        pirow = keep.tile([P, 2 * P], BF16, name="pirow")
        picol = keep.tile([P, PI_ROWS], F32, name="picol")
        pib = [keep.tile([P, D], BF16, name=f"pib{i}") for i in range(2)]
        id32 = keep.tile([P, P], F32, name="id32")
        warm = keep.tile([P, 2], F32, name="warm")

        def load_x(m, c0=0, c1=D):
            nc.sync.dma_start(out=x[m][:, c0:c1], in_=e0[m * P : (m + 1) * P, c0:c1])

        def load_words(s, g):
            nc.sync.dma_start(out=words[s][g][:].bitcast(I32), in_=words_in[s][g].bitcast(I32))

        def load_scales(s, g0=0, g1=GROUPS):
            for q in range(4):
                nc.sync.dma_start(
                    out=planes[s][32 * q : 32 * q + 4, g0:g1, :].bitcast(I32),
                    in_=scales_in[s][g0:g1, 4 * q : 4 * q + 4, :].rearrange("g q n -> q g n").bitcast(I32),
                )

        nc.vector.memset(pirow[:], 0.0)
        nc.vector.memset(warm[:], 0.0)
        nc.vector.memset(planes[0][:].rearrange("p g n -> p (g n)").bitcast(I32), 0)
        make_identity(nc, id32[:])
        nc.scalar.dma_start(out=pirow[0:PI_ROWS, :], in_=pi1.rearrange("(r c) -> r c", c=2 * P))
        nc.scalar.copy(out=warm[:, 1:2], in_=warm[:, 0:1])
        for s in (1, 2):
            nc.gpsimd.memset(planes[s][:].rearrange("p g n -> p (g n)").bitcast(I32), 0)
        load_x(0, 0, 512)
        load_x(0, 512, D)
        load_scales(0, 0, 1)
        load_words(0, 0)
        load_scales(0, 1, 3)
        load_words(0, 1)
        load_x(1)
        load_words(0, 2)
        load_x(2)
        load_scales(1)
        for g in range(GROUPS):
            load_words(1, g)
        load_x(3)
        nc.sync.dma_start(out=pib[1][:], in_=pi2.partition_broadcast(P))
        load_scales(2)
        for g in range(GROUPS):
            load_words(2, g)

        banks = {}

        def bank(key, dtype=F32):
            banks[key] = psum.tile([P, 512 if dtype == F32 else 1024], dtype, name=f"b_{key}", tag="bank")
            return banks[key]

        def cols(n):
            return slice(512 * n, 512 * (n + 1))

        def words_up(s, m, g, u):
            if s == 0 and m == 0:
                return x[m][:].bitcast(F32)[:, 256 * g + u : 256 * (g + 1) : 2]
            src = (xr, b1, b2)[s][m]
            return src[:].bitcast(F32)[:, 256 * g + 128 * u : 256 * g + 128 * (u + 1)]

        def turn(s, m, groups, key):
            if groups[0] == 0:
                grouped[s][m] = stage.tile([P, 12 * P], BF16, name=f"gr{s}_{m}", tag="gr", align_bytes=64)
            bk = bank(key)
            for i, (g, u) in enumerate([(g, u) for g in groups for u in range(2)]):
                nc.tensor.transpose(bk[:, P * i : P * (i + 1)], words_up(s, m, g, u), id32[:])

        def turn_out(s, m, groups, key, copy_on):
            k = len(groups)
            dst = grouped[s][m][:].bitcast(F32)[:, 256 * groups[0] : 256 * (groups[0] + k)]
            dst = dst.rearrange("p (s r u) -> p s r u", r=P, u=2)
            src = banks[key][:, : 256 * k].rearrange("p (s u r) -> p s r u", u=2, r=P)
            if copy_on == "S":
                nc.scalar.copy(out=dst, in_=src)
            else:
                nc.vector.tensor_copy(out=dst, in_=src)

        def quantise(s, m, groups):
            g, k = groups[0], len(groups)
            nc.vector.quantize_mx(
                out=codes[s][m][:, g * P : (g + k) * P].bitcast(FP8X4),
                scales=cscales[s][m][:, g * P : (g + k) * P],
                in_=grouped[s][m][:, 512 * g : 512 * (g + k)],
            )

        def one_pass(acc, s, m, n, g):
            nc.tensor.matmul_mx(
                out=acc[:],
                lhsT=codes[s][m][:, g * P : (g + 1) * P].bitcast(FP8X4),
                lhsT_scale=cscales[s][m][:, g * P : (g + 1) * P],
                rhs=words[s][g][:, 1024 * n : 1024 * (n + 1)].bitcast(FP4X4),
                rhs_scale=planes[s][:, g, cols(n)],
                start=(g == 0),
                stop=(g == GROUPS - 1),
            )

        def reorder(m):
            nc.scalar.copy(
                out=xr[m][:].bitcast(F32).rearrange("q (g u p) -> q g u p", g=GROUPS, u=2),
                in_=x[m][:].bitcast(F32).rearrange("q (g p u) -> q g u p", g=GROUPS, u=2),
            )

        def pi_columns():
            nc.tensor.transpose(bank("picol")[:, :P], pirow[:].bitcast(F32), id32[:])

        def pi_spread(key, r0, rn):
            bk = bank(key)
            for j in range(rn):
                c = r0 + j
                nc.tensor.transpose(bk[:, P * j : P * (j + 1)], picol[:, c : c + 1].to_broadcast([P, P]), id32[:])

        def pi_out(key, r0, rn):
            nc.scalar.copy(out=pib[0][:].bitcast(F32)[:, P * r0 : P * (r0 + rn)], in_=banks[key][:, : P * rn])

        def mul(eng, y, a, b, n):
            eng.tensor_tensor(out=y[:, cols(n)], in0=a[:, cols(n)], in1=b[:, cols(n)], op=MULT)

        def epi1(m, n):
            nc.vector.scalar_tensor_tensor(
                out=ne1[m][:, cols(n)], in0=banks[(1, m, n)][:], scalar=0.0, in1=y1[m][:, cols(n)], op0=MAX, op1=SUB
            )

        def cast1(m, n):
            nc.scalar.copy(
                out=b1[m][:, cols(n)].rearrange("q (u p e) -> q u p e", u=2, e=2),
                in_=ne1[m][:, cols(n)].rearrange("q (p u e) -> q u p e", u=2, e=2),
            )

        def epi2(m, n):
            acc = banks[(2, m, n)][:].rearrange("q (p u e) -> q u p e", u=2, e=2)
            y = y2[m][:, cols(n)].rearrange("q (p u e) -> q u p e", u=2, e=2)
            for u in range(2):
                c = 512 * n + 256 * u
                nc.vector.scalar_tensor_tensor(
                    out=b2[m][:, c : c + 256].rearrange("q (p e) -> q p e", e=2),
                    in0=acc[:, u],
                    scalar=0.0,
                    in1=y[:, u],
                    op0=MIN,
                    op1=SUB,
                )

        res = {}

        def epi3(m, n, c0, c1, eng, last):
            if (m, n) not in res:
                res[(m, n)] = stage.tile([P, 512], F32, name=f"res{m}_{n}", tag="res")
            r = res[(m, n)]
            if eng == "S":
                nc.scalar.copy(out=r[:, c0:c1], in_=banks[(3, m, n)][:, c0:c1])
            else:
                nc.vector.tensor_copy(out=r[:, c0:c1], in_=banks[(3, m, n)][:, c0:c1])
            if last:
                nc.sync.dma_start(out=out[m * P : (m + 1) * P, cols(n)], in_=r[:])

        def last_product(m, n):
            for h in range(2):
                acc = bank((3, m, n, h))
                for q in range(2):
                    c = 512 * n + 256 * h + P * q
                    for g in range(GROUPS):
                        nc.tensor.matmul_mx(
                            out=acc[:, P * q : P * (q + 1)],
                            lhsT=codes[2][m][:, g * P : (g + 1) * P].bitcast(FP8X4),
                            lhsT_scale=cscales[2][m][:, g * P : (g + 1) * P],
                            rhs=words[2][g][:, 2 * c : 2 * (c + P)].bitcast(FP4X4),
                            rhs_scale=planes[2][:, g, c : c + P],
                            start=(g == 0),
                            stop=(g == GROUPS - 1),
                        )

        def last_out(m, n, step):
            if step == 0:
                r = stage.tile([P, 256], F32, name="last0", tag="last")
                nc.vector.tensor_copy(out=r[:], in_=banks[(3, m, n, 0)][:, :256])
                nc.sync.dma_start(out=out[m * P : (m + 1) * P, 512 * n : 512 * n + 256], in_=r[:])
                res["last"] = stage.tile([P, 256], F32, name="last1", tag="last")
                nc.vector.tensor_copy(out=res["last"][:, :P], in_=banks[(3, m, n, 1)][:, :P])
            else:
                nc.scalar.copy(out=res["last"][:, P:], in_=banks[(3, m, n, 1)][:, P:256])
                nc.sync.dma_start(out=out[m * P : (m + 1) * P, 512 * n + 256 : 512 * n + 512], in_=res["last"][:])

        def product(s, m, n):
            if (s, m, n) == LAST:
                last_product(m, n)
                return
            acc = bank((s + 1, m, n))
            for g in range(GROUPS):
                one_pass(acc, s, m, n, g)

        def head(g):
            for n in range(NT):
                if g == 0:
                    bank((1, 0, n))
                one_pass(banks[(1, 0, n)], 0, 0, n, g)

        def do(name):
            if name == "picol":
                pi_columns()
            elif name == "cpc":
                nc.scalar.copy(out=picol[:], in_=banks["picol"][:, :PI_ROWS])
            elif name in ("pi0a", "pi0b"):
                pi_spread(name, *((0, 4) if name == "pi0a" else (4, 2)))
            elif name in ("cpia", "cpib"):
                pi_out("pi0" + name[3], *((0, 4) if name == "cpia" else (4, 2)))
            elif name in ("Ta", "Tb"):
                turn(0, 0, [0] if name == "Ta" else [1, 2], name)
            elif name in ("cTa", "cTb"):
                turn_out(0, 0, [0] if name == "cTa" else [1, 2], name[1:], ENGINE.get(name, "S"))
            elif name in ("qTa", "qTb"):
                quantise(0, 0, [0] if name == "qTa" else [1, 2])
            elif name.startswith("re"):
                reorder(int(name[2]))
            elif name.startswith("H"):
                head(int(name[3]))
            elif name.startswith("M"):
                product(*[int(v) for v in name[1:].split("_")])
            elif name.startswith("T"):
                s, m = int(name[1]), int(name[3])
                turn(s, m, [0, 1], name + "a")
                turn(s, m, [2], name + "b")
            elif name.startswith("ca"):
                cast1(int(name[2]), int(name[3]))
            elif name.startswith("c"):
                turn_out(int(name[1]), int(name[3]), [0, 1] if name[4] == "a" else [2], "T" + name[1:], ENGINE.get(name, "S"))
            elif name.startswith("q"):
                quantise(int(name[1]), int(name[3]), [0, 1] if name[4] == "a" else [2])
            elif name.startswith("ya"):
                m, n = int(name[2]), int(name[3])
                mul(nc.gpsimd if name in ENGINE else nc.vector, y1[m], x[m], pib[0], n)
            elif name.startswith("yb"):
                m, n = int(name[2]), int(name[3])
                mul(nc.gpsimd if name in ENGINE else nc.vector, y2[m], ne1[m], pib[1], n)
            elif name.startswith("s1"):
                epi1(int(name[3]), int(name[4]))
            elif name.startswith("s2"):
                epi2(int(name[3]), int(name[4]))
            elif name == "oS":
                last_out(LAST[1], LAST[2], 1)
            elif name == "oV":
                last_out(LAST[1], LAST[2], 0)
            else:
                epi3(int(name[1]), int(name[2]), 0, 512, ENGINE.get(name, "V"), True)

        for name in ORDER.split():
            do(name)
